import numpy as np
import ml_dtypes


def mxq(x, axis, fmt="e4m3"):
    dtype, down = {"e4m3": (ml_dtypes.float8_e4m3fn, 7), "e5m2": (ml_dtypes.float8_e5m2, 14)}[fmt]
    v = np.moveaxis(np.asarray(x, np.float32).astype(ml_dtypes.bfloat16).astype(np.float64), axis, -1)
    blocks = v.reshape(v.shape[:-1] + (-1, 32))
    amax = np.abs(blocks).max(-1, keepdims=True)
    byte = np.maximum(np.where(amax > 0, np.frexp(amax)[1] - 1 + 127, 0) - down, 1)
    scale = np.exp2(byte - 127.0)
    codes = (blocks / scale).astype(np.float32).astype(dtype).astype(np.float64)
    return np.moveaxis((codes * scale).reshape(v.shape), -1, axis)


WIDE = False


def mx_kscale(k):
    if not WIDE:
        return np.ones(k)
    levels = np.array([10, -10, 5, -5, 0])
    if k % 512:
        return np.exp2(np.random.permutation(np.resize(levels, k // 32))).repeat(32)
    a = np.empty((k // 512, 16))
    for p in range(k // 512):
        a[p, :8] = np.random.permutation(np.resize(levels, 8))
        for g in range(8):
            far = levels[np.abs(levels - a[p, g]) >= 10]
            a[p, g + 8] = far[np.random.randint(len(far))]
    return np.exp2(a.ravel()).repeat(32)


def f64(x):
    return np.asarray(x).astype(np.float64)


def striped(idx):
    return np.tile(np.asarray(idx).reshape(-1, 16).T, (8, 1)).astype(np.uint16)


def unstriped(offs):
    return offs[:16].T.reshape(-1).astype(np.int64)


E2M1 = np.array([0.0, 0.5, 1.0, 1.5, 2.0, 3.0, 4.0, 6.0, -0.0, -0.5, -1.0, -1.5, -2.0, -3.0, -4.0, -6.0])


def pack_weight(w, fmt):
    k, n = w.shape
    w = f64(np.asarray(w, np.float32).astype(ml_dtypes.bfloat16)).reshape(k // 32, 32, n)
    amax = np.abs(w).max(1)
    if fmt == "e4m3":
        byte = np.frexp(amax)[1] - 1 + 127 - 7
    else:
        mant, ex = np.frexp(amax / 6.0)
        byte = np.where(mant > 0.5, ex, ex - 1) + 127
    byte = np.clip(np.where(amax > 0, byte, 1), 1, 254)
    scaled = (w * np.exp2(127.0 - byte)[:, None, :]).reshape(k, n).astype(np.float32)
    by_word = np.ascontiguousarray(scaled.reshape(k // 512, 128, 4, n).transpose(0, 1, 3, 2))
    if fmt == "e4m3":
        words = by_word.astype(ml_dtypes.float8_e4m3fn).view(np.uint8)
    else:
        c = by_word.astype(ml_dtypes.float4_e2m1fn).view(np.uint8) & 0xF
        words = (c[..., 0::2] | (c[..., 1::2] << 4)).reshape(k // 512, 128, 2 * n)
    return np.ascontiguousarray(words), np.ascontiguousarray(byte.astype(np.uint8).reshape(k // 512, 16, n))


def unpack_weight(words, scales, fmt):
    g, _, n = scales.shape
    words = np.ascontiguousarray(words).reshape(g, 128, n, -1)
    if fmt == "e4m3":
        vals = words.view(ml_dtypes.float8_e4m3fn).astype(np.float64)
    else:
        nib = np.empty((g, 128, n, 4), np.uint8)
        nib[..., 0::2] = words & 0xF
        nib[..., 1::2] = words >> 4
        vals = E2M1[nib]
    vals = vals * np.repeat(np.exp2(scales.astype(np.float64) - 127.0), 8, axis=1)[..., None]
    return vals.transpose(0, 1, 3, 2).reshape(g * 512, n)


def sigmoid(v):
    return 1.0 / (1.0 + np.exp(-v))


def bf(x):
    return np.asarray(x, np.float32).astype(ml_dtypes.bfloat16)


def planes(Y):
    r, m = Y.shape
    b = f64(bf(Y)).reshape(r // 32, 32, m)
    amax = np.abs(b).max(1)
    byte = np.clip(np.where(amax > 0, np.frexp(amax)[1] - 1 + 127 - 7, 1), 1, 254)
    codes = (b * np.exp2(127.0 - byte)[:, None, :]).reshape(r, m).astype(np.float32).astype(ml_dtypes.float8_e4m3fn).view(np.uint8)
    words = codes.reshape(r // 512, 128, 4, m).transpose(0, 1, 3, 2)
    return np.ascontiguousarray(words), np.ascontiguousarray(byte.astype(np.uint8).reshape(r // 512, 16, m))


D, E, T, I, Q, G = 512, 512, 2048, 512, 256, 32


def setup_inputs():
    n = np.random.standard_normal
    idx = np.random.permutation(T)[:I]
    fd = mx_kscale(D)
    fe = mx_kscale(E)
    keysp = pack_weight(n((D, T)) / fd[:, None], "e2m1")
    valsp = pack_weight(n((E, T)) / fe[:, None], "e2m1")
    return {
        "query": (n((D, Q)) * 1.0 / np.sqrt(D) * fd[:, None]).astype(np.float32),
        "keys_words": keysp[0],
        "keys_scales": keysp[1],
        "steep": (np.random.uniform(1.0, 4.0, (I, 1))).astype(np.float32),
        "fs": (np.random.uniform(1.0, 4.0, (I, 1))).astype(np.float32),
        "gout": (n((E, Q)) * 1 / np.sqrt(E) * fe[:, None]).astype(np.float32),
        "vals_words": valsp[0],
        "vals_scales": valsp[1],
        "offs": striped(idx),
    }


def reference(query, keys_words, keys_scales, steep, fs, gout, vals_words, vals_scales, offs):
    idx = unstriped(offs)
    keysu = unpack_weight(keys_words, keys_scales, "e2m1")
    valsu = unpack_weight(vals_words, vals_scales, "e2m1")
    keysidxg = keysu[:, idx]
    queryq = mxq(f64(query), 0, "e4m3")
    a = keysidxg.T @ queryq
    b = a.reshape(I, G, Q // G).mean(axis=2)
    br = np.repeat(b, Q // G, axis=1)
    w = sigmoid((a - br) * f64(steep))
    valsidxg = valsu[:, idx]
    goutq = mxq(f64(gout), 0, "e4m3")
    dp = valsidxg.T @ goutq
    dz = dp * w * (1.0 - w) * f64(steep) * f64(fs)
    dm = dz.reshape(I, G, Q // G).mean(axis=2)
    dr = np.repeat(dm, Q // G, axis=1)
    y = dz - dr
    words, scales = planes(y)
    return y, words, scales

@@ -1,0 +1,181 @@
+from contextlib import ExitStack
+
+import concourse.mybir as mybir
+from concourse.masks import make_identity
+
+F32 = mybir.dt.float32
+BF16 = mybir.dt.bfloat16
+I32 = mybir.dt.int32
+U32 = mybir.dt.uint32
+U16 = mybir.dt.uint16
+U8 = mybir.dt.uint8
+FP8X4 = mybir.dt.float8_e4m3fn_x4
+FP4X4 = mybir.dt.float4_e2m1fn_x4
+ALU = mybir.AluOpType
+ACT = mybir.ActivationFunctionType
+AX = mybir.AxisListType
+
+P = 128
+PACK = 4
+T = 2048
+I = 512
+Q = 256
+TEAM = 8
+HALF = Q // 2
+FLOPS = 2 * 2 * 512 * I * Q
+
+
+def tile_attend_gteamcontrast_pl_kernel(tc, query, keys_words, keys_scales, steep, fs, gout, vals_words, vals_scales, offs, out_0, out_1, out_2):
+    nc = tc.nc
+    with ExitStack() as ctx:
+        sb = ctx.enter_context(tc.tile_pool(name="sb", bufs=1))
+        ps = ctx.enter_context(tc.psum_pool(name="ps", bufs=1))
+
+        def new(name, shape, dtype, tag=None):
+            return sb.tile(shape, dtype, name=name, tag=tag or name, align_bytes=64)
+
+        offsets = sb.tile([P, I // 16], U16, name="offsets")
+        nc.sync.dma_start(offsets[:], offs)
+
+        kw = new("kw", [P, T], U16)
+        ks = new("ks", [P, T], U8)
+        vs = new("vs", [P, T], U8)
+        q_raw = new("q_raw", [P, PACK, Q], F32)
+        st = new("st", [P, PACK], F32)
+        fst = new("fst", [P, PACK], F32)
+        warm_in = new("warm_in", [P, 8], F32, tag="late_vw")
+        warm_out = new("warm_out", [P, 8], F32, tag="late_g")
+
+        nc.vector.memset(ks[:].bitcast(I32), 0)
+        nc.vector.memset(warm_in[:], 0.0)
+        nc.vector.memset(vs[:].bitcast(I32), 0)
+
+        def load_scales(eng, tile, src):
+            for quad in range(4):
+                eng.dma_start(tile[32 * quad:32 * quad + 4, :].bitcast(I32), src[0, 4 * quad:4 * quad + 4, :].bitcast(I32))
+
+        nc.sync.dma_start(kw[:].bitcast(I32), keys_words[0].bitcast(I32))
+        nc.sync.dma_start(q_raw[:], query.rearrange("(p j) q -> p j q", j=PACK))
+        load_scales(nc.scalar, ks, keys_scales)
+        nc.scalar.activation(warm_out[:], warm_in[:], ACT.Tanh)
+        load_scales(nc.scalar, vs, vals_scales)
+        g_raw = new("g_raw", [P, PACK, Q], F32, tag="late_g")
+        vw = new("vw", [P, T], U16, tag="late_vw")
+        nc.sync.dma_start(vw[:].bitcast(I32), vals_words[0].bitcast(I32))
+        nc.sync.dma_start(g_raw[:], gout.rearrange("(p j) q -> p j q", j=PACK))
+        nc.gpsimd.dma_start(st[:], steep.rearrange("(p t) o -> p (t o)", t=PACK))
+        nc.gpsimd.dma_start(fst[:], fs.rearrange("(p t) o -> p (t o)", t=PACK))
+
+        half_st = new("half_st", [P, PACK], F32)
+        prod = new("prod", [P, PACK], F32)
+        coef = new("coef", [P, PACK], F32)
+        coef8 = new("coef8", [P, PACK], F32)
+        nc.gpsimd.tensor_scalar(half_st[:], st[:], 0.5, 0.0, ALU.mult, ALU.add)
+        nc.gpsimd.tensor_tensor(prod[:], st[:], fst[:], ALU.mult)
+        nc.gpsimd.tensor_scalar(coef[:], prod[:], -0.25, 0.0, ALU.mult, ALU.add)
+        nc.gpsimd.tensor_scalar(coef8[:], prod[:], -0.25 / TEAM, 0.0, ALU.mult, ALU.add)
+
+        def gather(name, pool_tile, dtype, tag=None):
+            got = new(name + "_got", [P, I], dtype, tag=tag)
+            nc.vector.tensor_copy(got[:], pool_tile[:].indirect(offsets[:]))
+            return got
+
+        def deal(name, got, dtype):
+            dealt = new(name + "_dealt", [P, PACK, P], dtype)
+            nc.vector.tensor_copy(dealt[:], got[:].rearrange("p (s t) -> p t s", t=PACK))
+            return dealt
+
+        def interleave(name, raw, tag):
+            grouped = new(name + "_bf", [P, Q, PACK], BF16, tag=tag)
+            nc.scalar.copy(grouped[:].rearrange("p (c i) j -> p c j i", i=4), raw[:].rearrange("p j (c i) -> p c j i", i=4))
+            return grouped
+
+        def quantize(name, grouped):
+            codes = new(name + "_codes", [P, Q], U32)
+            scales = new(name + "_scales", [P, Q], U8)
+            nc.vector.quantize_mx(out=codes[:].bitcast(FP8X4), scales=scales[:], in_=grouped[:].rearrange("p q j -> p (q j)"))
+            return codes, scales
+
+        def product(banks, words, scales, codes, code_scales):
+            for t in range(PACK):
+                nc.tensor.matmul_mx(out=banks[t // 2][:, t % 2, :], lhsT=words[:, t, :].bitcast(FP4X4), lhsT_scale=scales[:, t, :],
+                                    rhs=codes[:].bitcast(FP8X4), rhs_scale=code_scales[:], start=True, stop=True)
+
+        ident = new("ident", [P, P], F32)
+        make_identity(nc, ident[:])
+
+        ks_got = gather("ks", ks, U8)
+        kw_got = gather("kw", kw, U16)
+        q_bf = new("q_bf", [P, Q, PACK], BF16)
+        nc.scalar.copy(q_bf[:].rearrange("p (h g i) j -> p h g j i", h=2, i=4), q_raw[:].rearrange("p j (g h i) -> p h g j i", h=2, i=4))
+        q_codes, q_scales = quantize("q", q_bf)
+        at_ps = [ps.tile([P, I], F32, name="at_ps%d" % h) for h in range(2)]
+        at_sb = [new("at_sb%d" % h, [P, PACK, P], F32) for h in range(2)]
+        for h in range(2):
+            cols = slice(h * HALF, (h + 1) * HALF)
+            nc.tensor.matmul_mx(out=at_ps[h][:], lhsT=q_codes[:, cols].bitcast(FP8X4), lhsT_scale=q_scales[:, cols],
+                                rhs=kw_got[:].bitcast(FP4X4), rhs_scale=ks_got[:], start=True, stop=True)
+            nc.scalar.copy(at_sb[h][:], at_ps[h][:].rearrange("p (s t) -> p t s", t=PACK))
+        g_bf = interleave("g", g_raw, "kw_got")
+        vs_got = gather("vs", vs, U8)
+        vw_got = gather("vw", vw, U16, tag="q_bf")
+        vs_d = deal("vs", vs_got, U8)
+        vw_d = deal("vw", vw_got, U16)
+        g_codes, g_scales = quantize("g", g_bf)
+
+        G = Q // TEAM
+        a_ps = [ps.tile([P, 2, 2, HALF], F32, name="a_ps%d" % b) for b in range(2)]
+        pair = [ps.tile([P, 2, HALF], F32, name="pair%d" % b) for b in range(2)]
+        a_sum = [new("a_sum%d" % b, [P, 2 * G], F32) for b in range(2)]
+        z = [new("z%d" % b, [P, 2, Q], F32) for b in range(2)]
+        th = [new("th%d" % t, [P, Q], F32) for t in range(PACK)]
+        sq = [new("sq%d" % t, [P, Q], F32) for t in range(PACK)]
+        for b in range(2):
+            for e in range(2):
+                for h in range(2):
+                    nc.tensor.matmul(pair[b][:, e, :], lhsT=at_sb[h][:, 2 * b + e, :], rhs=ident[:], is_transpose=True, start=(h == 0), stop=(h == 1))
+            for e in range(2):
+                for h in range(2):
+                    nc.tensor.transpose(a_ps[b][:, h, e, :], at_sb[h][:, 2 * b + e, :], ident[:])
+        for b in range(2):
+            nc.vector.tensor_reduce(a_sum[b][:], pair[b][:].rearrange("p e (g i) -> p (e g) i", i=4), AX.X, ALU.add)
+            for h in range(2):
+                nc.vector.scalar_tensor_tensor(z[b][:].rearrange("p e (g h i) -> p h (e g) i", h=2, i=4)[:, h],
+                                               a_sum[b][:].unsqueeze(2).to_broadcast([P, 2 * G, 4]), -1.0 / TEAM,
+                                               a_ps[b][:, h].rearrange("p e (g i) -> p (e g) i", i=4), ALU.mult, ALU.add)
+        for t in range(PACK):
+            nc.scalar.activation(th[t][:], z[t // 2][:, t % 2, :], ACT.Tanh, scale=half_st[:, t:t + 1])
+            nc.scalar.activation(sq[t][:], th[t][:], ACT.Square)
+
+        dp_both = ps.tile([P, PACK, Q], F32, name="dp_both", tag="pair1")
+        dp_ps = [dp_both[:, 2 * b:2 * b + 2, :] for b in range(2)]
+        product(dp_ps, vw_d, vs_d, g_codes, g_scales)
+
+        u = [new("u%d" % t, [P, Q], F32) for t in range(PACK)]
+        u_sum = [new("u_sum%d" % b, [P, 2, G], F32) for b in range(2)]
+        cm = [new("cm%d" % b, [P, 2, G], F32) for b in range(2)]
+        y = new("y", [P, PACK, Q], F32)
+        y_bf = new("y_bf", [P, Q, PACK], BF16)
+        y_codes = new("y_codes", [P, Q], U32)
+        y_scales = new("y_scales", [P, Q], U8)
+        out_rows = out_0.rearrange("(p t) q -> p t q", t=PACK)
+        for b in range(2):
+            for t in (2 * b, 2 * b + 1):
+                nc.vector.scalar_tensor_tensor(u[t][:], sq[t][:], 1.0, dp_ps[b][:, t % 2, :], ALU.subtract, ALU.mult)
+            for t in (2 * b, 2 * b + 1):
+                nc.vector.tensor_reduce(u_sum[b][:, t % 2, :], u[t][:].rearrange("p (g r) -> p g r", r=TEAM), AX.X, ALU.add)
+            nc.vector.tensor_tensor(cm[b][:], u_sum[b][:], coef8[:, 2 * b:2 * b + 2].unsqueeze(2).to_broadcast([P, 2, G]), ALU.mult)
+        for b in range(2):
+            for t in (2 * b, 2 * b + 1):
+                nc.vector.scalar_tensor_tensor(y[:, t, :].rearrange("p (g r) -> p g r", r=TEAM),
+                                               u[t][:].rearrange("p (g r) -> p g r", r=TEAM), coef[:, t:t + 1],
+                                               cm[b][:, t % 2, :].unsqueeze(2).to_broadcast([P, G, TEAM]), ALU.mult, ALU.subtract)
+            nc.sync.dma_start(out_rows[:, 2 * b:2 * b + 2, :], y[:, 2 * b:2 * b + 2, :])
+        SPLIT = 96
+        for eng_copy, cols in ((nc.scalar.copy, slice(0, SPLIT)), (nc.vector.tensor_copy, slice(SPLIT, Q))):
+            eng_copy(y_bf[:, cols, :].rearrange("p (c i) j -> p c j i", i=4), y[:, :, cols].rearrange("p j (c i) -> p c j i", i=4))
+        nc.vector.quantize_mx(out=y_codes[:].bitcast(FP8X4), scales=y_scales[:], in_=y_bf[:].rearrange("p q j -> p (q j)"))
+        nc.sync.dma_start(out_1[0].rearrange("p c r -> p (c r)").bitcast(I32), y_codes[:].bitcast(I32))
+        for quad in range(4):
+            eng = nc.scalar if quad < 3 else nc.sync
+            eng.dma_start(out_2[0, 4 * quad:4 * quad + 4, :].bitcast(I32), y_scales[32 * quad:32 * quad + 4, :].bitcast(I32))

@@ -48,17 +48,15 @@ def tile_attend_gteamcontrast_pl_kernel(tc, query, keys_words, keys_scales, stee
 
         nc.vector.memset(ks[:].bitcast(I32), 0)
         nc.vector.memset(warm_in[:], 0.0)
-        nc.vector.memset(vs[:].bitcast(I32), 0)
 
         def load_scales(eng, tile, src):
             for quad in range(4):
                 eng.dma_start(tile[32 * quad:32 * quad + 4, :].bitcast(I32), src[0, 4 * quad:4 * quad + 4, :].bitcast(I32))
 
-        nc.sync.dma_start(kw[:].bitcast(I32), keys_words[0].bitcast(I32))
         nc.sync.dma_start(q_raw[:], query.rearrange("(p j) q -> p j q", j=PACK))
+        nc.sync.dma_start(kw[:].bitcast(I32), keys_words[0].bitcast(I32))
         load_scales(nc.scalar, ks, keys_scales)
         nc.scalar.activation(warm_out[:], warm_in[:], ACT.Tanh)
-        load_scales(nc.scalar, vs, vals_scales)
         g_raw = new("g_raw", [P, PACK, Q], F32, tag="late_g")
         vw = new("vw", [P, T], U16, tag="late_vw")
         nc.sync.dma_start(vw[:].bitcast(I32), vals_words[0].bitcast(I32))
@@ -66,14 +64,10 @@ def tile_attend_gteamcontrast_pl_kernel(tc, query, keys_words, keys_scales, stee
         nc.gpsimd.dma_start(st[:], steep.rearrange("(p t) o -> p (t o)", t=PACK))
         nc.gpsimd.dma_start(fst[:], fs.rearrange("(p t) o -> p (t o)", t=PACK))
 
-        half_st = new("half_st", [P, PACK], F32)
-        prod = new("prod", [P, PACK], F32)
-        coef = new("coef", [P, PACK], F32)
-        coef8 = new("coef8", [P, PACK], F32)
-        nc.gpsimd.tensor_scalar(half_st[:], st[:], 0.5, 0.0, ALU.mult, ALU.add)
-        nc.gpsimd.tensor_tensor(prod[:], st[:], fst[:], ALU.mult)
-        nc.gpsimd.tensor_scalar(coef[:], prod[:], -0.25, 0.0, ALU.mult, ALU.add)
-        nc.gpsimd.tensor_scalar(coef8[:], prod[:], -0.25 / TEAM, 0.0, ALU.mult, ALU.add)
+        ident = new("ident", [P, P], F32)
+        make_identity(nc, ident[:])
+        nc.gpsimd.memset(vs[:].bitcast(I32), 0)
+        load_scales(nc.sync, vs, vals_scales)
 
         def gather(name, pool_tile, dtype, tag=None):
             got = new(name + "_got", [P, I], dtype, tag=tag)
@@ -101,26 +95,25 @@ def tile_attend_gteamcontrast_pl_kernel(tc, query, keys_words, keys_scales, stee
                 nc.tensor.matmul_mx(out=banks[t // 2][:, t % 2, :], lhsT=words[:, t, :].bitcast(FP4X4), lhsT_scale=scales[:, t, :],
                                     rhs=codes[:].bitcast(FP8X4), rhs_scale=code_scales[:], start=True, stop=True)
 
-        ident = new("ident", [P, P], F32)
-        make_identity(nc, ident[:])
-
         ks_got = gather("ks", ks, U8)
-        kw_got = gather("kw", kw, U16)
         q_bf = new("q_bf", [P, Q, PACK], BF16)
         nc.scalar.copy(q_bf[:].rearrange("p (h g i) j -> p h g j i", h=2, i=4), q_raw[:].rearrange("p j (g h i) -> p h g j i", h=2, i=4))
         q_codes, q_scales = quantize("q", q_bf)
+        kw_got = gather("kw", kw, U16, tag="ks")
         at_ps = [ps.tile([P, I], F32, name="at_ps%d" % h) for h in range(2)]
         at_sb = [new("at_sb%d" % h, [P, PACK, P], F32) for h in range(2)]
         for h in range(2):
             cols = slice(h * HALF, (h + 1) * HALF)
             nc.tensor.matmul_mx(out=at_ps[h][:], lhsT=q_codes[:, cols].bitcast(FP8X4), lhsT_scale=q_scales[:, cols],
                                 rhs=kw_got[:].bitcast(FP4X4), rhs_scale=ks_got[:], start=True, stop=True)
-            nc.scalar.copy(at_sb[h][:], at_ps[h][:].rearrange("p (s t) -> p t s", t=PACK))
-        g_bf = interleave("g", g_raw, "kw_got")
-        vs_got = gather("vs", vs, U8)
+            nc.scalar.activation(at_sb[h][:], at_ps[h][:].rearrange("p (s t) -> p t s", t=PACK), ACT.Copy, scale=0.5)
+        g_bf = interleave("g", g_raw, "ks")
         vw_got = gather("vw", vw, U16, tag="q_bf")
-        vs_d = deal("vs", vs_got, U8)
+        vs_got = gather("vs", vs, U8, tag="kw")
+        coef = new("coef", [P, PACK], F32, tag="late_vw")
+        nc.vector.scalar_tensor_tensor(coef[:], st[:], -0.25, fst[:], ALU.mult, ALU.mult)
         vw_d = deal("vw", vw_got, U16)
+        vs_d = deal("vs", vs_got, U8)
         g_codes, g_scales = quantize("g", g_bf)
 
         G = Q // TEAM
@@ -144,7 +137,7 @@ def tile_attend_gteamcontrast_pl_kernel(tc, query, keys_words, keys_scales, stee
                                                a_sum[b][:].unsqueeze(2).to_broadcast([P, 2 * G, 4]), -1.0 / TEAM,
                                                a_ps[b][:, h].rearrange("p e (g i) -> p (e g) i", i=4), ALU.mult, ALU.add)
         for t in range(PACK):
-            nc.scalar.activation(th[t][:], z[t // 2][:, t % 2, :], ACT.Tanh, scale=half_st[:, t:t + 1])
+            nc.scalar.activation(th[t][:], z[t // 2][:, t % 2, :], ACT.Tanh, scale=st[:, t:t + 1])
             nc.scalar.activation(sq[t][:], th[t][:], ACT.Square)
 
         dp_both = ps.tile([P, PACK, Q], F32, name="dp_both", tag="pair1")
@@ -159,18 +152,37 @@ def tile_attend_gteamcontrast_pl_kernel(tc, query, keys_words, keys_scales, stee
         y_codes = new("y_codes", [P, Q], U32)
         y_scales = new("y_scales", [P, Q], U8)
         out_rows = out_0.rearrange("(p t) q -> p t q", t=PACK)
-        for b in range(2):
-            for t in (2 * b, 2 * b + 1):
-                nc.vector.scalar_tensor_tensor(u[t][:], sq[t][:], 1.0, dp_ps[b][:, t % 2, :], ALU.subtract, ALU.mult)
-            for t in (2 * b, 2 * b + 1):
-                nc.vector.tensor_reduce(u_sum[b][:, t % 2, :], u[t][:].rearrange("p (g r) -> p g r", r=TEAM), AX.X, ALU.add)
-            nc.vector.tensor_tensor(cm[b][:], u_sum[b][:], coef8[:, 2 * b:2 * b + 2].unsqueeze(2).to_broadcast([P, 2, G]), ALU.mult)
-        for b in range(2):
-            for t in (2 * b, 2 * b + 1):
-                nc.vector.scalar_tensor_tensor(y[:, t, :].rearrange("p (g r) -> p g r", r=TEAM),
-                                               u[t][:].rearrange("p (g r) -> p g r", r=TEAM), coef[:, t:t + 1],
-                                               cm[b][:, t % 2, :].unsqueeze(2).to_broadcast([P, G, TEAM]), ALU.mult, ALU.subtract)
-            nc.sync.dma_start(out_rows[:, 2 * b:2 * b + 2, :], y[:, 2 * b:2 * b + 2, :])
+
+        def weigh(t):
+            nc.vector.scalar_tensor_tensor(u[t][:], sq[t][:], 1.0, dp_ps[t // 2][:, t % 2, :], ALU.subtract, ALU.mult)
+
+        def team_sum(t):
+            nc.vector.tensor_reduce(u_sum[t // 2][:, t % 2, :], u[t][:].rearrange("p (g r) -> p g r", r=TEAM), AX.X, ALU.add)
+
+        def team_mean(b):
+            nc.vector.scalar_tensor_tensor(cm[b][:], u_sum[b][:], 1.0 / TEAM, coef[:, 2 * b:2 * b + 2].unsqueeze(2).to_broadcast([P, 2, G]), ALU.mult, ALU.mult)
+
+        def centre(t):
+            nc.vector.scalar_tensor_tensor(y[:, t, :].rearrange("p (g r) -> p g r", r=TEAM),
+                                           u[t][:].rearrange("p (g r) -> p g r", r=TEAM), coef[:, t:t + 1],
+                                           cm[t // 2][:, t % 2, :].unsqueeze(2).to_broadcast([P, G, TEAM]), ALU.mult, ALU.subtract)
+
+        weigh(0)
+        weigh(1)
+        team_sum(0)
+        team_sum(1)
+        weigh(2)
+        team_mean(0)
+        weigh(3)
+        team_sum(2)
+        team_sum(3)
+        centre(0)
+        team_mean(1)
+        centre(1)
+        nc.sync.dma_start(out_rows[:, 0:2, :], y[:, 0:2, :])
+        centre(2)
+        centre(3)
+        nc.sync.dma_start(out_rows[:, 2:4, :], y[:, 2:4, :])
         SPLIT = 96
         for eng_copy, cols in ((nc.scalar.copy, slice(0, SPLIT)), (nc.vector.tensor_copy, slice(SPLIT, Q))):
             eng_copy(y_bf[:, cols, :].rearrange("p (c i) j -> p c j i", i=4), y[:, :, cols].rearrange("p j (c i) -> p c j i", i=4))

@@ -39,35 +39,37 @@ def tile_attend_gteamcontrast_pl_kernel(tc, query, keys_words, keys_scales, stee
 
         kw = new("kw", [P, T], U16)
         ks = new("ks", [P, T], U8)
-        vs = new("vs", [P, T], U8)
         q_raw = new("q_raw", [P, PACK, Q], F32)
         st = new("st", [P, PACK], F32)
         fst = new("fst", [P, PACK], F32)
-        warm_in = new("warm_in", [P, 8], F32, tag="late_vw")
-        warm_out = new("warm_out", [P, 8], F32, tag="late_g")
+        warm_in = new("warm_in", [P, 1], F32, tag="late_vw")
+        warm_bias = new("warm_bias", [P, 1], F32, tag="late_g")
+        zero_bias = new("zero_bias", [P, 1], F32)
+        vs = new("vs", [P, T], U8)
 
         nc.vector.memset(ks[:].bitcast(I32), 0)
         nc.vector.memset(warm_in[:], 0.0)
+        nc.vector.memset(warm_bias[:], 0.0)
+        nc.vector.memset(vs[:].bitcast(I32), 0)
 
         def load_scales(eng, tile, src):
             for quad in range(4):
                 eng.dma_start(tile[32 * quad:32 * quad + 4, :].bitcast(I32), src[0, 4 * quad:4 * quad + 4, :].bitcast(I32))
 
-        nc.sync.dma_start(q_raw[:], query.rearrange("(p j) q -> p j q", j=PACK))
         nc.sync.dma_start(kw[:].bitcast(I32), keys_words[0].bitcast(I32))
+        nc.sync.dma_start(q_raw[:], query.rearrange("(p j) q -> p j q", j=PACK))
         load_scales(nc.scalar, ks, keys_scales)
-        nc.scalar.activation(warm_out[:], warm_in[:], ACT.Tanh)
-        g_raw = new("g_raw", [P, PACK, Q], F32, tag="late_g")
+        nc.scalar.activation(zero_bias[:], warm_in[:], ACT.Tanh, bias=warm_bias[:])
+        load_scales(nc.scalar, vs, vals_scales)
         vw = new("vw", [P, T], U16, tag="late_vw")
         nc.sync.dma_start(vw[:].bitcast(I32), vals_words[0].bitcast(I32))
+        g_raw = new("g_raw", [P, PACK, Q], F32, tag="late_g")
         nc.sync.dma_start(g_raw[:], gout.rearrange("(p j) q -> p j q", j=PACK))
         nc.gpsimd.dma_start(st[:], steep.rearrange("(p t) o -> p (t o)", t=PACK))
         nc.gpsimd.dma_start(fst[:], fs.rearrange("(p t) o -> p (t o)", t=PACK))
 
         ident = new("ident", [P, P], F32)
         make_identity(nc, ident[:])
-        nc.gpsimd.memset(vs[:].bitcast(I32), 0)
-        load_scales(nc.sync, vs, vals_scales)
 
         def gather(name, pool_tile, dtype, tag=None):
             got = new(name + "_got", [P, I], dtype, tag=tag)
@@ -95,11 +97,11 @@ def tile_attend_gteamcontrast_pl_kernel(tc, query, keys_words, keys_scales, stee
                 nc.tensor.matmul_mx(out=banks[t // 2][:, t % 2, :], lhsT=words[:, t, :].bitcast(FP4X4), lhsT_scale=scales[:, t, :],
                                     rhs=codes[:].bitcast(FP8X4), rhs_scale=code_scales[:], start=True, stop=True)
 
+        kw_got = gather("kw", kw, U16)
         ks_got = gather("ks", ks, U8)
         q_bf = new("q_bf", [P, Q, PACK], BF16)
         nc.scalar.copy(q_bf[:].rearrange("p (h g i) j -> p h g j i", h=2, i=4), q_raw[:].rearrange("p j (g h i) -> p h g j i", h=2, i=4))
         q_codes, q_scales = quantize("q", q_bf)
-        kw_got = gather("kw", kw, U16, tag="ks")
         at_ps = [ps.tile([P, I], F32, name="at_ps%d" % h) for h in range(2)]
         at_sb = [new("at_sb%d" % h, [P, PACK, P], F32) for h in range(2)]
         for h in range(2):
@@ -107,40 +109,48 @@ def tile_attend_gteamcontrast_pl_kernel(tc, query, keys_words, keys_scales, stee
             nc.tensor.matmul_mx(out=at_ps[h][:], lhsT=q_codes[:, cols].bitcast(FP8X4), lhsT_scale=q_scales[:, cols],
                                 rhs=kw_got[:].bitcast(FP4X4), rhs_scale=ks_got[:], start=True, stop=True)
             nc.scalar.activation(at_sb[h][:], at_ps[h][:].rearrange("p (s t) -> p t s", t=PACK), ACT.Copy, scale=0.5)
-        g_bf = interleave("g", g_raw, "ks")
+        g_bf = interleave("g", g_raw, "kw_got")
+        vs_got = gather("vs", vs, U8)
         vw_got = gather("vw", vw, U16, tag="q_bf")
-        vs_got = gather("vs", vs, U8, tag="kw")
         coef = new("coef", [P, PACK], F32, tag="late_vw")
         nc.vector.scalar_tensor_tensor(coef[:], st[:], -0.25, fst[:], ALU.mult, ALU.mult)
-        vw_d = deal("vw", vw_got, U16)
         vs_d = deal("vs", vs_got, U8)
+        vw_d = deal("vw", vw_got, U16)
         g_codes, g_scales = quantize("g", g_bf)
 
         G = Q // TEAM
         a_ps = [ps.tile([P, 2, 2, HALF], F32, name="a_ps%d" % b) for b in range(2)]
-        pair = [ps.tile([P, 2, HALF], F32, name="pair%d" % b) for b in range(2)]
+        pair = ps.tile([P, 2, HALF], F32, name="pair")
         a_sum = [new("a_sum%d" % b, [P, 2 * G], F32) for b in range(2)]
         z = [new("z%d" % b, [P, 2, Q], F32) for b in range(2)]
         th = [new("th%d" % t, [P, Q], F32) for t in range(PACK)]
         sq = [new("sq%d" % t, [P, Q], F32) for t in range(PACK)]
-        for b in range(2):
-            for e in range(2):
-                for h in range(2):
-                    nc.tensor.matmul(pair[b][:, e, :], lhsT=at_sb[h][:, 2 * b + e, :], rhs=ident[:], is_transpose=True, start=(h == 0), stop=(h == 1))
+
+        def turn_scores(b):
             for e in range(2):
                 for h in range(2):
                     nc.tensor.transpose(a_ps[b][:, h, e, :], at_sb[h][:, 2 * b + e, :], ident[:])
-        for b in range(2):
-            nc.vector.tensor_reduce(a_sum[b][:], pair[b][:].rearrange("p e (g i) -> p (e g) i", i=4), AX.X, ALU.add)
+
+        def subtract_mean(b):
             for h in range(2):
                 nc.vector.scalar_tensor_tensor(z[b][:].rearrange("p e (g h i) -> p h (e g) i", h=2, i=4)[:, h],
                                                a_sum[b][:].unsqueeze(2).to_broadcast([P, 2 * G, 4]), -1.0 / TEAM,
                                                a_ps[b][:, h].rearrange("p e (g i) -> p (e g) i", i=4), ALU.mult, ALU.add)
+
+        turn_scores(0)
+        for e in range(2):
+            for h in range(2):
+                nc.tensor.matmul(pair[:, e, :], lhsT=at_sb[h][:, 2 + e, :], rhs=ident[:], is_transpose=True, start=(h == 0), stop=(h == 1))
+        turn_scores(1)
+        nc.vector.tensor_reduce(a_sum[0][:], a_ps[0][:].rearrange("p h e (g i) -> p (e g) h i", i=4), AX.XY, ALU.add)
+        subtract_mean(0)
+        nc.vector.tensor_reduce(a_sum[1][:], pair[:].rearrange("p e (g i) -> p (e g) i", i=4), AX.X, ALU.add)
+        subtract_mean(1)
         for t in range(PACK):
-            nc.scalar.activation(th[t][:], z[t // 2][:, t % 2, :], ACT.Tanh, scale=st[:, t:t + 1])
+            nc.scalar.activation(th[t][:], z[t // 2][:, t % 2, :], ACT.Tanh, bias=zero_bias[:], scale=st[:, t:t + 1])
             nc.scalar.activation(sq[t][:], th[t][:], ACT.Square)
 
-        dp_both = ps.tile([P, PACK, Q], F32, name="dp_both", tag="pair1")
+        dp_both = ps.tile([P, PACK, Q], F32, name="dp_both", tag="pair")
         dp_ps = [dp_both[:, 2 * b:2 * b + 2, :] for b in range(2)]
         product(dp_ps, vw_d, vs_d, g_codes, g_scales)
 

from contextlib import ExitStack

import concourse.mybir as mybir
from concourse.masks import make_identity

F32 = mybir.dt.float32
BF16 = mybir.dt.bfloat16
I32 = mybir.dt.int32
U32 = mybir.dt.uint32
U16 = mybir.dt.uint16
U8 = mybir.dt.uint8
FP8X4 = mybir.dt.float8_e4m3fn_x4
FP4X4 = mybir.dt.float4_e2m1fn_x4
ALU = mybir.AluOpType
ACT = mybir.ActivationFunctionType
AX = mybir.AxisListType

P = 128
PACK = 4
T = 2048
I = 512
Q = 256
TEAM = 8
HALF = Q // 2
FLOPS = 2 * 2 * 512 * I * Q


def tile_attend_gteamcontrast_pl_kernel(tc, query, keys_words, keys_scales, steep, fs, gout, vals_words, vals_scales, offs, out_0, out_1, out_2):
    nc = tc.nc
    with ExitStack() as ctx:
        sb = ctx.enter_context(tc.tile_pool(name="sb", bufs=1))
        ps = ctx.enter_context(tc.psum_pool(name="ps", bufs=1))

        def new(name, shape, dtype, tag=None):
            return sb.tile(shape, dtype, name=name, tag=tag or name, align_bytes=64)

        offsets = sb.tile([P, I // 16], U16, name="offsets")
        nc.sync.dma_start(offsets[:], offs)

        kw = new("kw", [P, T], U16)
        ks = new("ks", [P, T], U8)
        q_raw = new("q_raw", [P, PACK, Q], F32)
        st = new("st", [P, PACK], F32)
        fst = new("fst", [P, PACK], F32)
        warm_in = new("warm_in", [P, 1], F32, tag="late_vw")
        warm_bias = new("warm_bias", [P, 1], F32, tag="late_g")
        zero_bias = new("zero_bias", [P, 1], F32)
        vs = new("vs", [P, T], U8)

        nc.vector.memset(ks[:].bitcast(I32), 0)
        nc.vector.memset(warm_in[:], 0.0)
        nc.vector.memset(warm_bias[:], 0.0)
        nc.vector.memset(vs[:].bitcast(I32), 0)

        def load_scales(eng, tile, src):
            for quad in range(4):
                eng.dma_start(tile[32 * quad:32 * quad + 4, :].bitcast(I32), src[0, 4 * quad:4 * quad + 4, :].bitcast(I32))

        nc.sync.dma_start(kw[:].bitcast(I32), keys_words[0].bitcast(I32))
        nc.sync.dma_start(q_raw[:], query.rearrange("(p j) q -> p j q", j=PACK))
        load_scales(nc.scalar, ks, keys_scales)
        nc.scalar.activation(zero_bias[:], warm_in[:], ACT.Tanh, bias=warm_bias[:])
        load_scales(nc.scalar, vs, vals_scales)
        vw = new("vw", [P, T], U16, tag="late_vw")
        nc.sync.dma_start(vw[:].bitcast(I32), vals_words[0].bitcast(I32))
        g_raw = new("g_raw", [P, PACK, Q], F32, tag="late_g")
        nc.sync.dma_start(g_raw[:], gout.rearrange("(p j) q -> p j q", j=PACK))
        nc.gpsimd.dma_start(st[:], steep.rearrange("(p t) o -> p (t o)", t=PACK))
        nc.gpsimd.dma_start(fst[:], fs.rearrange("(p t) o -> p (t o)", t=PACK))

        ident = new("ident", [P, P], F32)
        make_identity(nc, ident[:])

        def gather(name, pool_tile, dtype, tag=None):
            got = new(name + "_got", [P, I], dtype, tag=tag)
            nc.vector.tensor_copy(got[:], pool_tile[:].indirect(offsets[:]))
            return got

        def deal(name, got, dtype):
            dealt = new(name + "_dealt", [P, PACK, P], dtype)
            nc.vector.tensor_copy(dealt[:], got[:].rearrange("p (s t) -> p t s", t=PACK))
            return dealt

        def interleave(name, raw, tag):
            grouped = new(name + "_bf", [P, Q, PACK], BF16, tag=tag)
            nc.scalar.copy(grouped[:].rearrange("p (c i) j -> p c j i", i=4), raw[:].rearrange("p j (c i) -> p c j i", i=4))
            return grouped

        def quantize(name, grouped):
            codes = new(name + "_codes", [P, Q], U32)
            scales = new(name + "_scales", [P, Q], U8)
            nc.vector.quantize_mx(out=codes[:].bitcast(FP8X4), scales=scales[:], in_=grouped[:].rearrange("p q j -> p (q j)"))
            return codes, scales

        def product(banks, words, scales, codes, code_scales):
            for t in range(PACK):
                nc.tensor.matmul_mx(out=banks[t // 2][:, t % 2, :], lhsT=words[:, t, :].bitcast(FP4X4), lhsT_scale=scales[:, t, :],
                                    rhs=codes[:].bitcast(FP8X4), rhs_scale=code_scales[:], start=True, stop=True)

        kw_got = gather("kw", kw, U16)
        ks_got = gather("ks", ks, U8)
        q_bf = new("q_bf", [P, Q, PACK], BF16)
        nc.scalar.copy(q_bf[:].rearrange("p (h g i) j -> p h g j i", h=2, i=4), q_raw[:].rearrange("p j (g h i) -> p h g j i", h=2, i=4))
        q_codes, q_scales = quantize("q", q_bf)
        at_ps = [ps.tile([P, I], F32, name="at_ps%d" % h) for h in range(2)]
        at_sb = [new("at_sb%d" % h, [P, PACK, P], F32) for h in range(2)]
        for h in range(2):
            cols = slice(h * HALF, (h + 1) * HALF)
            nc.tensor.matmul_mx(out=at_ps[h][:], lhsT=q_codes[:, cols].bitcast(FP8X4), lhsT_scale=q_scales[:, cols],
                                rhs=kw_got[:].bitcast(FP4X4), rhs_scale=ks_got[:], start=True, stop=True)
            nc.scalar.activation(at_sb[h][:], at_ps[h][:].rearrange("p (s t) -> p t s", t=PACK), ACT.Copy, scale=0.5)
        g_bf = interleave("g", g_raw, "kw_got")
        vs_got = gather("vs", vs, U8)
        vw_got = gather("vw", vw, U16, tag="q_bf")
        coef = new("coef", [P, PACK], F32, tag="late_vw")
        nc.vector.scalar_tensor_tensor(coef[:], st[:], -0.25, fst[:], ALU.mult, ALU.mult)
        vs_d = deal("vs", vs_got, U8)
        vw_d = deal("vw", vw_got, U16)
        g_codes, g_scales = quantize("g", g_bf)

        G = Q // TEAM
        a_ps = [ps.tile([P, 2, 2, HALF], F32, name="a_ps%d" % b) for b in range(2)]
        pair = ps.tile([P, 2, HALF], F32, name="pair")
        a_sum = [new("a_sum%d" % b, [P, 2 * G], F32) for b in range(2)]
        z = [new("z%d" % b, [P, 2, Q], F32) for b in range(2)]
        th = [new("th%d" % t, [P, Q], F32) for t in range(PACK)]
        sq = [new("sq%d" % t, [P, Q], F32) for t in range(PACK)]

        def turn_scores(b):
            for e in range(2):
                for h in range(2):
                    nc.tensor.transpose(a_ps[b][:, h, e, :], at_sb[h][:, 2 * b + e, :], ident[:])

        def subtract_mean(b):
            for h in range(2):
                nc.vector.scalar_tensor_tensor(z[b][:].rearrange("p e (g h i) -> p h (e g) i", h=2, i=4)[:, h],
                                               a_sum[b][:].unsqueeze(2).to_broadcast([P, 2 * G, 4]), -1.0 / TEAM,
                                               a_ps[b][:, h].rearrange("p e (g i) -> p (e g) i", i=4), ALU.mult, ALU.add)

        turn_scores(0)
        for e in range(2):
            for h in range(2):
                nc.tensor.matmul(pair[:, e, :], lhsT=at_sb[h][:, 2 + e, :], rhs=ident[:], is_transpose=True, start=(h == 0), stop=(h == 1))
        turn_scores(1)
        nc.vector.tensor_reduce(a_sum[0][:], a_ps[0][:].rearrange("p h e (g i) -> p (e g) h i", i=4), AX.XY, ALU.add)
        subtract_mean(0)
        nc.vector.tensor_reduce(a_sum[1][:], pair[:].rearrange("p e (g i) -> p (e g) i", i=4), AX.X, ALU.add)
        subtract_mean(1)
        for t in range(PACK):
            nc.scalar.activation(th[t][:], z[t // 2][:, t % 2, :], ACT.Tanh, bias=zero_bias[:], scale=st[:, t:t + 1])
            nc.scalar.activation(sq[t][:], th[t][:], ACT.Square)

        dp_both = ps.tile([P, PACK, Q], F32, name="dp_both", tag="pair")
        dp_ps = [dp_both[:, 2 * b:2 * b + 2, :] for b in range(2)]
        product(dp_ps, vw_d, vs_d, g_codes, g_scales)

        u = [new("u%d" % t, [P, Q], F32) for t in range(PACK)]
        u_sum = [new("u_sum%d" % b, [P, 2, G], F32) for b in range(2)]
        cm = [new("cm%d" % b, [P, 2, G], F32) for b in range(2)]
        y = new("y", [P, PACK, Q], F32)
        y_bf = new("y_bf", [P, Q, PACK], BF16)
        y_codes = new("y_codes", [P, Q], U32)
        y_scales = new("y_scales", [P, Q], U8)
        out_rows = out_0.rearrange("(p t) q -> p t q", t=PACK)

        def weigh(t):
            nc.vector.scalar_tensor_tensor(u[t][:], sq[t][:], 1.0, dp_ps[t // 2][:, t % 2, :], ALU.subtract, ALU.mult)

        def team_sum(t):
            nc.vector.tensor_reduce(u_sum[t // 2][:, t % 2, :], u[t][:].rearrange("p (g r) -> p g r", r=TEAM), AX.X, ALU.add)

        def team_mean(b):
            nc.vector.scalar_tensor_tensor(cm[b][:], u_sum[b][:], 1.0 / TEAM, coef[:, 2 * b:2 * b + 2].unsqueeze(2).to_broadcast([P, 2, G]), ALU.mult, ALU.mult)

        def centre(t):
            nc.vector.scalar_tensor_tensor(y[:, t, :].rearrange("p (g r) -> p g r", r=TEAM),
                                           u[t][:].rearrange("p (g r) -> p g r", r=TEAM), coef[:, t:t + 1],
                                           cm[t // 2][:, t % 2, :].unsqueeze(2).to_broadcast([P, G, TEAM]), ALU.mult, ALU.subtract)

        weigh(0)
        weigh(1)
        team_sum(0)
        team_sum(1)
        weigh(2)
        team_mean(0)
        weigh(3)
        team_sum(2)
        team_sum(3)
        centre(0)
        team_mean(1)
        centre(1)
        nc.sync.dma_start(out_rows[:, 0:2, :], y[:, 0:2, :])
        centre(2)
        centre(3)
        nc.sync.dma_start(out_rows[:, 2:4, :], y[:, 2:4, :])
        SPLIT = 96
        for eng_copy, cols in ((nc.scalar.copy, slice(0, SPLIT)), (nc.vector.tensor_copy, slice(SPLIT, Q))):
            eng_copy(y_bf[:, cols, :].rearrange("p (c i) j -> p c j i", i=4), y[:, :, cols].rearrange("p j (c i) -> p c j i", i=4))
        nc.vector.quantize_mx(out=y_codes[:].bitcast(FP8X4), scales=y_scales[:], in_=y_bf[:].rearrange("p q j -> p (q j)"))
        nc.sync.dma_start(out_1[0].rearrange("p c r -> p (c r)").bitcast(I32), y_codes[:].bitcast(I32))
        for quad in range(4):
            eng = nc.scalar if quad < 3 else nc.sync
            eng.dma_start(out_2[0, 4 * quad:4 * quad + 4, :].bitcast(I32), y_scales[32 * quad:32 * quad + 4, :].bitcast(I32))
